import numpy as np
import ml_dtypes


def mxq(x, axis, fmt="e4m3"):
    dtype, down = {"e4m3": (ml_dtypes.float8_e4m3fn, 7), "e5m2": (ml_dtypes.float8_e5m2, 14)}[fmt]
    v = np.moveaxis(np.asarray(x, np.float32).astype(ml_dtypes.bfloat16).astype(np.float64), axis, -1)
    blocks = v.reshape(v.shape[:-1] + (-1, 32))
    amax = np.abs(blocks).max(-1, keepdims=True)
    byte = np.maximum(np.where(amax > 0, np.frexp(amax)[1] - 1 + 127, 0) - down, 1)
    scale = np.exp2(byte - 127.0)
    codes = (blocks / scale).astype(np.float32).astype(dtype).astype(np.float64)
    return np.moveaxis((codes * scale).reshape(v.shape), -1, axis)


WIDE = False


def mx_kscale(k):
    if not WIDE:
        return np.ones(k)
    levels = np.array([10, -10, 5, -5, 0])
    if k % 512:
        return np.exp2(np.random.permutation(np.resize(levels, k // 32))).repeat(32)
    a = np.empty((k // 512, 16))
    for p in range(k // 512):
        a[p, :8] = np.random.permutation(np.resize(levels, 8))
        for g in range(8):
            far = levels[np.abs(levels - a[p, g]) >= 10]
            a[p, g + 8] = far[np.random.randint(len(far))]
    return np.exp2(a.ravel()).repeat(32)


def f64(x):
    return np.asarray(x).astype(np.float64)


def striped(idx):
    return np.tile(idx.reshape(-1, 16).T, (8, 1)).astype(np.uint16)


def unstriped(offs):
    return offs[:16].T.reshape(-1).astype(np.int64)


def pack_weight(w):
    k, n = w.shape
    w = f64(np.asarray(w, np.float32).astype(ml_dtypes.bfloat16)).reshape(k // 32, 32, n)
    amax = np.abs(w).max(1)
    byte = np.clip(np.where(amax > 0, np.frexp(amax)[1] - 1 + 127 - 7, 1), 1, 254)
    scaled = (w * np.exp2(127.0 - byte)[:, None, :]).reshape(k, n).astype(np.float32)
    words = np.ascontiguousarray(scaled.reshape(k // 512, 128, 4, n).transpose(0, 1, 3, 2)).astype(ml_dtypes.float8_e4m3fn).view(np.uint8)
    return words, np.ascontiguousarray(byte.astype(np.uint8).reshape(k // 512, 16, n))


def unpack_weight(words, scales):
    g, p, n, _ = words.shape
    vals = np.ascontiguousarray(words).view(ml_dtypes.float8_e4m3fn).astype(np.float64) * np.repeat(np.exp2(scales.astype(np.float64) - 127.0), 8, axis=1)[..., None]
    return vals.transpose(0, 1, 3, 2).reshape(g * 512, n)

def planes(y):
    n, m = y.shape
    v = y.astype(np.float32).astype(ml_dtypes.bfloat16).astype(np.float64).reshape(n // 32, 32, m)
    top = np.abs(v).max(1)
    byte = np.clip(np.where(top > 0, np.frexp(top)[1] - 1 + 127 - 7, 1), 1, 254)
    codes = (v * np.exp2(127.0 - byte)[:, None, :]).reshape(n, m).astype(np.float32).astype(ml_dtypes.float8_e4m3fn).view(np.uint8)
    words = codes.reshape(n // 512, 128, 4, m).transpose(0, 1, 3, 2)
    return np.ascontiguousarray(words), np.ascontiguousarray(byte.astype(np.uint8).reshape(n // 512, 16, m))


K, T, S, D, H = 512, 1024, 512, 4, 512


def setup_inputs():
    n = np.random.standard_normal
    s = mx_kscale(K)[:, None]
    u = mx_kscale(H)
    packed_xT = pack_weight(n((K, T)) * s)
    packed_w2 = pack_weight(n((H, H)) / np.sqrt(H) / u[:, None])
    return {
        "x_words": packed_xT[0],
        "x_scales": packed_xT[1],
        "w1": (n((K, H)) / np.sqrt(K) / s * u).astype(np.float32),
        "w2_words": packed_w2[0],
        "w2_scales": packed_w2[1],
        "taps": (n((H, D)) / np.sqrt(D)).astype(np.float32),
        "offs": striped(np.random.permutation(T)[:S]),
    }


def reference(x_words, x_scales, w1, w2_words, w2_scales, taps, offs):
    xq = unpack_weight(x_words, x_scales)[:, unstriped(offs)]
    h = mxq(f64(w1), 0, "e4m3").T @ xq
    z = f64(taps)[:, 0:1] * h + f64(taps)[:, 1:2] * (np.pad(h, ((0, 0), (1, 0)))[:, :S]) + f64(taps)[:, 2:3] * (np.pad(h, ((0, 0), (2, 0)))[:, :S]) + f64(taps)[:, 3:4] * (np.pad(h, ((0, 0), (3, 0)))[:, :S])
    out_0 = unpack_weight(w2_words, w2_scales).T @ mxq(z, 0, "e4m3")
    return (out_0,) + planes(out_0)

from contextlib import ExitStack

import concourse.mybir as mybir

K, T, S, D, H = 512, 1024, 512, 4, 512
FLOPS = 2 * K * H * S + 2 * H * H * S

F32 = mybir.dt.float32
BF16 = mybir.dt.bfloat16
I32 = mybir.dt.int32
U32 = mybir.dt.uint32
U16 = mybir.dt.uint16
U8 = mybir.dt.uint8
FP8X4 = mybir.dt.float8_e4m3fn_x4
COPY = mybir.ActivationFunctionType.Copy
MULT = mybir.AluOpType.mult
ADD = mybir.AluOpType.add

P = 128
PACK = 4
WIDTHS = (128, 128, 128, 128)
SUM_ON = ("g", "g", "g", "v")
ROUND_ON = ("v", "v", "v", "v")
SCALAR_M = 20
HALO = 8


def tile_picked_dconv_none_po_kernel(
    tc, x_words, x_scales, w1, w2_words, w2_scales, taps, offs, out_0, out_1, out_2
):
    nc = tc.nc
    with ExitStack() as ctx:
        keep = ctx.enter_context(tc.tile_pool(name="keep", bufs=1))
        hps = ctx.enter_context(tc.psum_pool(name="hps", bufs=4))
        ops = ctx.enter_context(tc.psum_pool(name="ops", bufs=4))

        offsets = keep.tile([P, S // 16], U16, name="offsets")
        nc.sync.dma_start(offsets[:], offs)

        xs = keep.tile([P, T], U8, name="xs", align_bytes=64)
        nc.gpsimd.memset(xs[:].bitcast(I32), 0)

        w1_rows = w1.rearrange("(p j) c -> p j c", j=PACK)
        w1_half = []
        for a in range(2):
            raw = keep.tile([P, PACK, H // 2], F32, name=f"w1raw{a}", tag=f"raw{a}", align_bytes=64)
            nc.sync.dma_start(raw[:], w1_rows[:, :, a * (H // 2) : (a + 1) * (H // 2)])
            w1_half.append(raw)
            if a == 0:
                for q in range(4):
                    nc.sync.dma_start(xs[32 * q : 32 * q + 4, :].bitcast(I32), x_scales[0, 4 * q : 4 * q + 4, :].bitcast(I32))

        xw = keep.tile([P, T], U32, name="xw", align_bytes=64)
        nc.sync.dma_start(xw[:].bitcast(I32), x_words[0].rearrange("p n t -> p (n t)").bitcast(I32))

        tap = keep.tile([P, PACK * D], F32, name="tap")
        nc.gpsimd.dma_start(tap[:], taps.rearrange("(p t) d -> p (t d)", t=PACK))

        w2s = keep.tile([P, H], U8, name="w2s", align_bytes=64)
        nc.gpsimd.memset(w2s[:].bitcast(I32), 0)
        for q in range(4):
            nc.gpsimd.dma_start(w2s[32 * q : 32 * q + 4, :].bitcast(I32), w2_scales[0, 4 * q : 4 * q + 4, :].bitcast(I32))

        nears = [keep.tile([P, PACK, w + HALO], F32, name=f"near{c}") for c, w in enumerate(WIDTHS)]
        fars = [keep.tile([P, PACK, w + HALO], F32, name=f"far{c}") for c, w in enumerate(WIDTHS)]
        nc.vector.memset(nears[0][:, :, 0:1], 0.0)
        nc.vector.memset(fars[0][:, :, 0:3], 0.0)

        gs = keep.tile([P, S], U8, name="gs", align_bytes=64)
        nc.vector.tensor_copy(gs[:], xs[:].indirect(offsets[:]))

        w1b = keep.tile([P, PACK, P, PACK], BF16, name="w1b", align_bytes=64)

        def w1_views(a, m0, m1):
            src = w1_half[a][:, :, PACK * m0 : PACK * m1].rearrange("p j (m t) -> p m j t", t=PACK)
            dst = w1b[:, :, 64 * a + m0 : 64 * a + m1, :].rearrange("p t m j -> p m j t")
            return dst, src

        dst, src = w1_views(0, 0, 64)
        nc.scalar.activation(dst, src, COPY)
        w2w = keep.tile([P, H], U32, name="w2w", tag="raw0", align_bytes=64)
        nc.sync.dma_start(w2w[:].bitcast(I32), w2_words[0].rearrange("p n t -> p (n t)").bitcast(I32))
        dst, src = w1_views(1, 0, SCALAR_M)
        nc.scalar.activation(dst, src, COPY)
        dst, src = w1_views(1, SCALAR_M, 64)
        nc.vector.tensor_copy(dst, src)
        w1c = keep.tile([P, H], U32, name="w1c", align_bytes=64)
        w1s = keep.tile([P, H], U8, name="w1s", align_bytes=64)
        nc.vector.quantize_mx(out=w1c[:].bitcast(FP8X4), scales=w1s[:], in_=w1b[:].rearrange("p t m j -> p (t m j)"))

        starts = [sum(WIDTHS[:c]) for c in range(len(WIDTHS))]
        gw = []
        for c, (j0, w) in enumerate(zip(starts, WIDTHS)):
            g = keep.tile([P, w], U32, name=f"gw{c}", align_bytes=64)
            nc.vector.tensor_copy(g[:], xw[:].indirect(offsets[:, j0 // 16 : (j0 + w) // 16]))
            gw.append(g)

        w2wd = keep.tile([P, H], U32, name="w2wd", align_bytes=64)
        w2sd = keep.tile([P, H], U8, name="w2sd", align_bytes=64)
        nc.vector.tensor_copy(w2wd[:].rearrange("p (t m) -> p m t", t=PACK), w2w[:].rearrange("p (m t) -> p m t", t=PACK))
        nc.gpsimd.tensor_copy(w2sd[:].rearrange("p (t m) -> p t m", t=PACK), w2s[:].rearrange("p (m t) -> p t m", t=PACK))

        oc = keep.tile([P, S], U32, name="oc", align_bytes=64)
        osc = keep.tile([P, S], U8, name="osc", align_bytes=64)
        out_rows = out_0.rearrange("(p t) j -> p t j", t=PACK)
        words_out = out_1[0].rearrange("p n t -> p (n t)").bitcast(I32)

        for c, (j0, w) in enumerate(zip(starts, WIDTHS)):
            j1 = j0 + w
            last = c == len(WIDTHS) - 1
            near, far = nears[c], fars[c]
            per_bank = max(1, 256 // w)
            for t0 in range(0, PACK, per_bank):
                h = hps.tile([P, per_bank, w], F32, name="h")
                ts = range(t0, t0 + per_bank)
                for t in ts:
                    cols = slice(P * t, P * (t + 1))
                    nc.tensor.matmul_mx(
                        out=h[:, t - t0, :], lhsT=w1c[:, cols].bitcast(FP8X4), lhsT_scale=w1s[:, cols],
                        rhs=gw[c][:].bitcast(FP8X4), rhs_scale=gs[:, j0:j1], start=True, stop=True,
                    )
                for acc, d in ((near, 1), (far, 3)):
                    for t in ts:
                        n = w - d if last else w
                        nc.scalar.activation(acc[:, t, d : d + n], h[:, t - t0, 0:n], COPY, scale=tap[:, D * t + d : D * t + d + 1])
                order = ((near, 0), (far, 2)) if t0 + per_bank < PACK else ((far, 2), (near, 0))
                for acc, d in order:
                    for t in ts:
                        n = w - d if last else w
                        part = acc[:, t, d : d + n]
                        nc.vector.scalar_tensor_tensor(part, h[:, t - t0, 0:n], tap[:, D * t + d : D * t + d + 1], part, MULT, ADD)
            if not last:
                nc.scalar.activation(nears[c + 1][:, :, 0:1], near[:, :, w : w + 1], COPY)
                nc.vector.tensor_copy(fars[c + 1][:, :, 0:3], far[:, :, w : w + 3])

            zb = keep.tile([P, w, PACK], BF16, name=f"zb{c}", align_bytes=64)
            adder = nc.gpsimd if SUM_ON[c] == "g" else nc.vector
            adder.tensor_tensor(
                zb[:].rearrange("p (c i) t -> p c t i", i=4),
                near[:, :, 0:w].rearrange("p t (c i) -> p c t i", i=4),
                far[:, :, 0:w].rearrange("p t (c i) -> p c t i", i=4),
                ADD,
            )
            zc = keep.tile([P, w], U32, name=f"zc{c}", align_bytes=64)
            zs = keep.tile([P, w], U8, name=f"zs{c}", align_bytes=64)
            nc.vector.quantize_mx(out=zc[:].bitcast(FP8X4), scales=zs[:], in_=zb[:].rearrange("p j t -> p (j t)"))

            y = keep.tile([P, PACK, w], F32, name=f"y{c}")
            per_bank = 2 if (last or w == 256) else 4
            for t0 in range(0, PACK, per_bank):
                o = ops.tile([P, per_bank, w], F32, name="o")
                for t in range(t0, t0 + per_bank):
                    cols = slice(P * t, P * (t + 1))
                    nc.tensor.matmul_mx(
                        out=o[:, t - t0, :], lhsT=w2wd[:, cols].bitcast(FP8X4), lhsT_scale=w2sd[:, cols],
                        rhs=zc[:].bitcast(FP8X4), rhs_scale=zs[:], start=True, stop=True,
                    )
                if last and t0 > 0:
                    nc.vector.tensor_copy(y[:, t0 : t0 + per_bank, :], o[:])
                else:
                    nc.scalar.activation(y[:, t0 : t0 + per_bank, :], o[:], COPY)
            nc.sync.dma_start(out_rows[:, :, j0:j1], y[:])

            yb = keep.tile([P, w, PACK], BF16, name=f"yb{c}", align_bytes=64)
            rounder = nc.gpsimd if ROUND_ON[c] == "g" else nc.vector
            rounder.tensor_copy(yb[:].rearrange("p (c i) t -> p c t i", i=4), y[:].rearrange("p t (c i) -> p c t i", i=4))
            nc.vector.quantize_mx(out=oc[:, j0:j1].bitcast(FP8X4), scales=osc[:, j0:j1], in_=yb[:].rearrange("p j t -> p (j t)"))
            nc.sync.dma_start(words_out[:, j0:j1], oc[:, j0:j1].bitcast(I32))

        for q in range(4):
            queue = nc.scalar if q % 2 == 0 else nc.sync
            queue.dma_start(out_2[0, 4 * q : 4 * q + 4, :].bitcast(I32), osc[32 * q : 32 * q + 4, :].bitcast(I32))
